import numpy as np
import ml_dtypes


def mxq(x, axis, fmt="e4m3"):
    dtype, down = {"e4m3": (ml_dtypes.float8_e4m3fn, 7), "e5m2": (ml_dtypes.float8_e5m2, 14)}[fmt]
    v = np.moveaxis(np.asarray(x, np.float32).astype(ml_dtypes.bfloat16).astype(np.float64), axis, -1)
    blocks = v.reshape(v.shape[:-1] + (-1, 32))
    amax = np.abs(blocks).max(-1, keepdims=True)
    byte = np.maximum(np.where(amax > 0, np.frexp(amax)[1] - 1 + 127, 0) - down, 1)
    scale = np.exp2(byte - 127.0)
    codes = (blocks / scale).astype(np.float32).astype(dtype).astype(np.float64)
    return np.moveaxis((codes * scale).reshape(v.shape), -1, axis)


WIDE = False


def mx_kscale(k):
    if not WIDE:
        return np.ones(k)
    levels = np.array([30, -30])
    if k % 512:
        return np.exp2(np.random.permutation(np.resize(levels, k // 32))).repeat(32)
    a = np.empty((k // 512, 16))
    for p in range(k // 512):
        a[p, :8] = np.random.permutation(np.resize(levels, 8))
        for g in range(8):
            far = levels[np.abs(levels - a[p, g]) >= 10]
            a[p, g + 8] = far[np.random.randint(len(far))]
    return np.exp2(a.ravel()).repeat(32)


def f64(x):
    return np.asarray(x).astype(np.float64)


def striped(idx):
    return np.tile(np.asarray(idx).reshape(-1, 16).T, (8, 1)).astype(np.uint16)


def unstriped(offs):
    return offs[:16].T.reshape(-1).astype(np.int64)


K, N, T, S, J, I = 512, 512, 1024, 1024, 512, 512


def setup_inputs():
    n = np.random.standard_normal
    idx = np.random.permutation(T)[:J]
    idx2 = np.random.permutation(S)[:I]
    fj = mx_kscale(J)
    fi = mx_kscale(I)
    tj = np.ones(T)
    tj[idx] = fj
    ti = np.ones(S)
    ti[idx2] = fi
    return {
        "xa": (n((K, T)) * tj).astype(np.float32),
        "ga": (n((N, T)) * np.exp(0.5 * n((1, T))) / tj).astype(np.float32),
        "xb": (n((K, S)) * ti).astype(np.float32),
        "gb": (n((N, S)) / ti).astype(np.float32),
        "offs": striped(idx),
        "offs2": striped(idx2),
    }


def reference(xa, ga, xb, gb, offs, offs2):
    idx = unstriped(offs)
    idx2 = unstriped(offs2)
    x1 = f64(xa)[:, idx].T
    g1 = f64(ga)[:, idx].T
    x2 = f64(xb)[:, idx2].T
    g2 = f64(gb)[:, idx2].T
    x1q = mxq(x1, 0, "e4m3")
    g1q = mxq(g1, 0, "e5m2")
    x2q = mxq(x2, 0, "e4m3")
    g2q = mxq(g2, 0, "e4m3")
    w = x1q.T @ g1q + x2q.T @ g2q
    y = 0.04 * w
    return y

@@ -1,0 +1,161 @@
+from contextlib import ExitStack
+
+import concourse.mybir as mybir
+from concourse.masks import make_identity
+
+K, N, T, J = 512, 512, 1024, 512
+FLOPS = 2 * 2 * J * K * N
+
+F32 = mybir.dt.float32
+BF16 = mybir.dt.bfloat16
+U32 = mybir.dt.uint32
+U16 = mybir.dt.uint16
+U8 = mybir.dt.uint8
+E4M3 = mybir.dt.float8_e4m3fn_x4
+E5M2 = mybir.dt.float8_e5m2_x4
+COPY = mybir.ActivationFunctionType.Copy
+
+P = 128
+PACK = 4
+BLOCKS = 4
+OUT_SCALE = 0.04
+
+
+def tile_list_wgrad_two_batches_kernel(tc, xa, ga, xb, gb, offs, offs2, out):
+    nc = tc.nc
+
+    with ExitStack() as ctx:
+        keep = ctx.enter_context(tc.tile_pool(name="keep", bufs=1))
+        psum_t = ctx.enter_context(tc.psum_pool(name="psum_t", bufs=4))
+        psum_o = ctx.enter_context(tc.psum_pool(name="psum_o", bufs=1))
+
+        def sbuf(name, width, dtype, after=None):
+            return keep.tile([P, width], dtype, name=name, tag=after or name, align_bytes=64)
+
+        list_a = keep.tile([P, J // 16], U16, name="list_a")
+        list_b = keep.tile([P, J // 16], U16, name="list_b")
+        built = sbuf("built", P, F32)
+        make_identity(nc, built[:])
+        identity = sbuf("identity", P, F32)
+        nc.scalar.activation(identity[:], built[:], COPY)
+
+        sources = [(ga, r, list_a) for r in range(BLOCKS)] + [(gb, r, list_b) for r in range(BLOCKS)]
+        for r in range(BLOCKS):
+            sources.extend([(xa, r, list_a), (xb, r, list_b)])
+
+        rows = []
+        for i, (source, r, offsets) in enumerate(sources):
+            rows.append(sbuf(f"rows{i}", T, F32))
+            nc.sync.dma_start(out=rows[i][:], in_=source[r * P : (r + 1) * P, :])
+            if i == 0:
+                nc.sync.dma_start(list_a[:], offs)
+            if i == 2:
+                nc.sync.dma_start(list_b[:], offs2)
+
+        rounded, picked, banks = {}, {}, {}
+
+        def order(tile):
+            return tile[:].rearrange("p (u b s) -> p b u s", u=2, s=16)
+
+        def cast(i):
+            rounded[i] = sbuf(f"rounded{i}", T, BF16)
+            nc.vector.tensor_copy(rounded[i][:], rows[i][:])
+
+        def gather_scalar(i):
+            picked[i] = sbuf(f"picked{i}", J, BF16)
+            nc.scalar.activation(order(picked[i]), rounded[i][:].indirect(sources[i][2][:]), COPY)
+
+        def gather_vector(i):
+            picked[i] = sbuf(f"picked{i}", J, BF16)
+            nc.vector.tensor_copy(order(picked[i]), rows[i][:].indirect(sources[i][2][:]))
+
+        def turn(tiles):
+            bank = psum_t.tile([P, 2, 2, P], F32, name="bank")
+            banks[tiles] = bank
+            for slot, i in enumerate(tiles):
+                words = picked[i][:].bitcast(F32)
+                for u in range(2):
+                    nc.tensor.transpose(bank[:, slot, u, :], words[:, u * P : (u + 1) * P], identity[:])
+
+        def weave(tiles, grouped):
+            nc.scalar.copy(
+                grouped.bitcast(F32).rearrange("p (i c u) -> p i c u", i=len(tiles), u=2),
+                banks[tiles][:, 0 : len(tiles)].rearrange("p i u c -> p i c u"),
+            )
+
+        def quantise(name, grouped, fmt, after=None):
+            width = grouped.shape[1] // PACK
+            codes = sbuf(f"codes_{name}", width, U32, after)
+            scales = sbuf(f"scales_{name}", width, U8)
+            nc.vector.quantize_mx(out=codes[:].bitcast(fmt), scales=scales[:], in_=grouped[:])
+            return codes[:].bitcast(fmt), scales[:]
+
+        accs = [psum_o.tile([P, N], F32, name=f"acc{m}") for m in range(BLOCKS)]
+
+        def multiply(m, batch, x, cols, g):
+            nc.tensor.matmul_mx(
+                out=accs[m][:],
+                lhsT=x[0][:, cols],
+                lhsT_scale=x[1][:, cols],
+                rhs=g[0],
+                rhs_scale=g[1],
+                start=(batch == 0),
+                stop=(batch == 1),
+            )
+
+        def emit(m, on_scalar, after=None):
+            result = sbuf(f"result{m}", N, F32, after)
+            if on_scalar:
+                nc.scalar.activation(result[:], accs[m][:], COPY, scale=OUT_SCALE)
+            else:
+                nc.vector.tensor_scalar_mul(result[:], accs[m][:], OUT_SCALE)
+            nc.sync.dma_start(out=out[m * P : (m + 1) * P, :], in_=result[:])
+
+        half = 2 * P * PACK
+        grouped, quantised = {}, {}
+        pairs = len(sources) // 2
+        last = pairs - 1
+
+        def weave_pair(p):
+            tiles = (2 * p, 2 * p + 1)
+            after = f"rounded{2 * p + 2}"
+            if p >= 4:
+                grouped[p] = sbuf(f"grouped{p}", half, BF16, after)
+                weave(tiles, grouped[p][:])
+            else:
+                if p % 2 == 0:
+                    grouped[p // 2] = sbuf(f"grouped{p // 2}", 2 * half, BF16, after)
+                weave(tiles, grouped[p // 2][:, (p % 2) * half : (p % 2 + 1) * half])
+
+        def quantise_pair(p, after):
+            if p >= 4:
+                x = quantise(f"x{p}", grouped[p], E4M3, after)
+                for batch in range(2):
+                    multiply(p - 4, batch, x, slice(batch * P, (batch + 1) * P), quantised[batch])
+            elif p % 2 == 1:
+                quantised[p // 2] = quantise(f"g{p // 2}", grouped[p // 2], (E5M2, E4M3)[p // 2], after)
+
+        for p in range(pairs):
+            cast(2 * p)
+            if p >= 2:
+                quantise_pair(p - 2, f"rows{2 * p}")
+            if p == last:
+                emit(0, True)
+            gather_scalar(2 * p)
+            if p >= 1:
+                weave_pair(p - 1)
+            gather_vector(2 * p + 1)
+            if p < last:
+                turn((2 * p, 2 * p + 1))
+
+        emit(1, False, f"rows{2 * last + 1}")
+        quantise_pair(last - 1, None)
+        for batch in range(2):
+            i = 2 * last + batch
+            turn((i,))
+            grouped[i] = sbuf(f"grouped_last{batch}", P * PACK, BF16)
+            weave((i,), grouped[i][:])
+            x = quantise(f"last{batch}", grouped[i], E4M3)
+            multiply(BLOCKS - 1, batch, x, slice(0, P), quantised[batch])
+        emit(2, False, "grouped_last1")
+        emit(3, True)

@@ -29,15 +29,22 @@ def tile_list_wgrad_two_batches_kernel(tc, xa, ga, xb, gb, offs, offs2, out):
         psum_t = ctx.enter_context(tc.psum_pool(name="psum_t", bufs=4))
         psum_o = ctx.enter_context(tc.psum_pool(name="psum_o", bufs=1))
 
+        placed = ctx.enter_context(tc.tile_pool(name="placed", bufs=1))
+
+        def place(name, width, dtype, i, half_index):
+            return placed.tile([P, width], dtype, name=name, align_bytes=64, offset=i * 4 * T + half_index * 2 * T)
+
         def sbuf(name, width, dtype, after=None):
             return keep.tile([P, width], dtype, name=name, tag=after or name, align_bytes=64)
 
         list_a = keep.tile([P, J // 16], U16, name="list_a")
         list_b = keep.tile([P, J // 16], U16, name="list_b")
-        built = sbuf("built", P, F32)
-        make_identity(nc, built[:])
+        seed = sbuf("seed", 8, F32)
+        nc.vector.memset(seed[:], 0.0)
+        warmed = sbuf("warmed", 8, F32)
+        nc.scalar.activation(warmed[:], seed[:], COPY)
         identity = sbuf("identity", P, F32)
-        nc.scalar.activation(identity[:], built[:], COPY)
+        make_identity(nc, identity[:])
 
         sources = [(ga, r, list_a) for r in range(BLOCKS)] + [(gb, r, list_b) for r in range(BLOCKS)]
         for r in range(BLOCKS):
@@ -45,7 +52,7 @@ def tile_list_wgrad_two_batches_kernel(tc, xa, ga, xb, gb, offs, offs2, out):
 
         rows = []
         for i, (source, r, offsets) in enumerate(sources):
-            rows.append(sbuf(f"rows{i}", T, F32))
+            rows.append(place(f"rows{i}", T, F32, i, 0))
             nc.sync.dma_start(out=rows[i][:], in_=source[r * P : (r + 1) * P, :])
             if i == 0:
                 nc.sync.dma_start(list_a[:], offs)
@@ -83,12 +90,8 @@ def tile_list_wgrad_two_batches_kernel(tc, xa, ga, xb, gb, offs, offs2, out):
                 banks[tiles][:, 0 : len(tiles)].rearrange("p i u c -> p i c u"),
             )
 
-        def quantise(name, grouped, fmt, after=None):
-            width = grouped.shape[1] // PACK
-            codes = sbuf(f"codes_{name}", width, U32, after)
-            scales = sbuf(f"scales_{name}", width, U8)
-            nc.vector.quantize_mx(out=codes[:].bitcast(fmt), scales=scales[:], in_=grouped[:])
-            return codes[:].bitcast(fmt), scales[:]
+        def quantise(codes, scales, grouped, fmt):
+            nc.vector.quantize_mx(out=codes.bitcast(fmt), scales=scales, in_=grouped)
 
         accs = [psum_o.tile([P, N], F32, name=f"acc{m}") for m in range(BLOCKS)]
 
@@ -117,30 +120,29 @@ def tile_list_wgrad_two_batches_kernel(tc, xa, ga, xb, gb, offs, offs2, out):
         last = pairs - 1
 
         def weave_pair(p):
-            tiles = (2 * p, 2 * p + 1)
-            after = f"rounded{2 * p + 2}"
-            if p >= 4:
-                grouped[p] = sbuf(f"grouped{p}", half, BF16, after)
-                weave(tiles, grouped[p][:])
-            else:
-                if p % 2 == 0:
-                    grouped[p // 2] = sbuf(f"grouped{p // 2}", 2 * half, BF16, after)
-                weave(tiles, grouped[p // 2][:, (p % 2) * half : (p % 2 + 1) * half])
+            grouped[p] = place(f"grouped{p}", half, BF16, 2 * p + 2, 1)[:]
+            weave((2 * p, 2 * p + 1), grouped[p])
 
-        def quantise_pair(p, after):
+        def quantise_pair(p, host):
             if p >= 4:
-                x = quantise(f"x{p}", grouped[p], E4M3, after)
+                codes = host[:, 0 : 2 * P]
+                scales = sbuf(f"scales{p}", 2 * P, U8)
+                quantise(codes, scales[:], grouped[p], E4M3)
                 for batch in range(2):
-                    multiply(p - 4, batch, x, slice(batch * P, (batch + 1) * P), quantised[batch])
+                    multiply(p - 4, batch, (codes.bitcast(E4M3), scales[:]), slice(batch * P, (batch + 1) * P), quantised[batch])
             elif p % 2 == 1:
-                quantised[p // 2] = quantise(f"g{p // 2}", grouped[p // 2], (E5M2, E4M3)[p // 2], after)
+                fmt = (E5M2, E4M3)[p // 2]
+                codes = host[:, 0:N]
+                scales = sbuf(f"scales{p}", N, U8)
+                for h in range(2):
+                    cols = slice(h * N // 2, (h + 1) * N // 2)
+                    quantise(codes[:, cols], scales[:, cols], grouped[p - 1 + h], fmt)
+                quantised[p // 2] = (codes.bitcast(fmt), scales[:])
 
         for p in range(pairs):
             cast(2 * p)
-            if p >= 2:
-                quantise_pair(p - 2, f"rows{2 * p}")
-            if p == last:
-                emit(0, True)
+            if p in (3, 5, 6, 7):
+                quantise_pair(p - 2, place(f"codes{p - 2}", N, U32, 2 * p, 0))
             gather_scalar(2 * p)
             if p >= 1:
                 weave_pair(p - 1)
@@ -148,14 +150,17 @@ def tile_list_wgrad_two_batches_kernel(tc, xa, ga, xb, gb, offs, offs2, out):
             if p < last:
                 turn((2 * p, 2 * p + 1))
 
-        emit(1, False, f"rows{2 * last + 1}")
-        quantise_pair(last - 1, None)
+        emit(0, False, f"rounded{2 * last}")
+        quantise_pair(last - 1, sbuf("codes_late", 2 * P, U32))
         for batch in range(2):
             i = 2 * last + batch
             turn((i,))
             grouped[i] = sbuf(f"grouped_last{batch}", P * PACK, BF16)
             weave((i,), grouped[i][:])
-            x = quantise(f"last{batch}", grouped[i], E4M3)
-            multiply(BLOCKS - 1, batch, x, slice(0, P), quantised[batch])
+            codes = sbuf(f"codes_last{batch}", P, U32)
+            scales = sbuf(f"scales_last{batch}", P, U8)
+            quantise(codes[:], scales[:], grouped[i][:], E4M3)
+            multiply(BLOCKS - 1, batch, (codes[:].bitcast(E4M3), scales[:]), slice(0, P), quantised[batch])
+        emit(1, True, f"picked{2 * last + 1}")
         emit(2, False, "grouped_last1")
         emit(3, True)

from contextlib import ExitStack

import concourse.mybir as mybir
from concourse.masks import make_identity

K, N, T, J = 512, 512, 1024, 512
FLOPS = 2 * 2 * J * K * N

F32 = mybir.dt.float32
BF16 = mybir.dt.bfloat16
U32 = mybir.dt.uint32
U16 = mybir.dt.uint16
U8 = mybir.dt.uint8
E4M3 = mybir.dt.float8_e4m3fn_x4
E5M2 = mybir.dt.float8_e5m2_x4
COPY = mybir.ActivationFunctionType.Copy

P = 128
PACK = 4
BLOCKS = 4
OUT_SCALE = 0.04


def tile_list_wgrad_two_batches_kernel(tc, xa, ga, xb, gb, offs, offs2, out):
    nc = tc.nc

    with ExitStack() as ctx:
        keep = ctx.enter_context(tc.tile_pool(name="keep", bufs=1))
        psum_t = ctx.enter_context(tc.psum_pool(name="psum_t", bufs=4))
        psum_o = ctx.enter_context(tc.psum_pool(name="psum_o", bufs=1))

        placed = ctx.enter_context(tc.tile_pool(name="placed", bufs=1))

        def place(name, width, dtype, i, half_index):
            return placed.tile([P, width], dtype, name=name, align_bytes=64, offset=i * 4 * T + half_index * 2 * T)

        def sbuf(name, width, dtype, after=None):
            return keep.tile([P, width], dtype, name=name, tag=after or name, align_bytes=64)

        list_a = keep.tile([P, J // 16], U16, name="list_a")
        list_b = keep.tile([P, J // 16], U16, name="list_b")
        seed = sbuf("seed", 8, F32)
        nc.vector.memset(seed[:], 0.0)
        warmed = sbuf("warmed", 8, F32)
        nc.scalar.activation(warmed[:], seed[:], COPY)
        identity = sbuf("identity", P, F32)
        make_identity(nc, identity[:])

        sources = [(ga, r, list_a) for r in range(BLOCKS)] + [(gb, r, list_b) for r in range(BLOCKS)]
        for r in range(BLOCKS):
            sources.extend([(xa, r, list_a), (xb, r, list_b)])

        rows = []
        for i, (source, r, offsets) in enumerate(sources):
            rows.append(place(f"rows{i}", T, F32, i, 0))
            nc.sync.dma_start(out=rows[i][:], in_=source[r * P : (r + 1) * P, :])
            if i == 0:
                nc.sync.dma_start(list_a[:], offs)
            if i == 2:
                nc.sync.dma_start(list_b[:], offs2)

        rounded, picked, banks = {}, {}, {}

        def order(tile):
            return tile[:].rearrange("p (u b s) -> p b u s", u=2, s=16)

        def cast(i):
            rounded[i] = sbuf(f"rounded{i}", T, BF16)
            nc.vector.tensor_copy(rounded[i][:], rows[i][:])

        def gather_scalar(i):
            picked[i] = sbuf(f"picked{i}", J, BF16)
            nc.scalar.activation(order(picked[i]), rounded[i][:].indirect(sources[i][2][:]), COPY)

        def gather_vector(i):
            picked[i] = sbuf(f"picked{i}", J, BF16)
            nc.vector.tensor_copy(order(picked[i]), rows[i][:].indirect(sources[i][2][:]))

        def turn(tiles):
            bank = psum_t.tile([P, 2, 2, P], F32, name="bank")
            banks[tiles] = bank
            for slot, i in enumerate(tiles):
                words = picked[i][:].bitcast(F32)
                for u in range(2):
                    nc.tensor.transpose(bank[:, slot, u, :], words[:, u * P : (u + 1) * P], identity[:])

        def weave(tiles, grouped):
            nc.scalar.copy(
                grouped.bitcast(F32).rearrange("p (i c u) -> p i c u", i=len(tiles), u=2),
                banks[tiles][:, 0 : len(tiles)].rearrange("p i u c -> p i c u"),
            )

        def quantise(codes, scales, grouped, fmt):
            nc.vector.quantize_mx(out=codes.bitcast(fmt), scales=scales, in_=grouped)

        accs = [psum_o.tile([P, N], F32, name=f"acc{m}") for m in range(BLOCKS)]

        def multiply(m, batch, x, cols, g):
            nc.tensor.matmul_mx(
                out=accs[m][:],
                lhsT=x[0][:, cols],
                lhsT_scale=x[1][:, cols],
                rhs=g[0],
                rhs_scale=g[1],
                start=(batch == 0),
                stop=(batch == 1),
            )

        def emit(m, on_scalar, after=None):
            result = sbuf(f"result{m}", N, F32, after)
            if on_scalar:
                nc.scalar.activation(result[:], accs[m][:], COPY, scale=OUT_SCALE)
            else:
                nc.vector.tensor_scalar_mul(result[:], accs[m][:], OUT_SCALE)
            nc.sync.dma_start(out=out[m * P : (m + 1) * P, :], in_=result[:])

        half = 2 * P * PACK
        grouped, quantised = {}, {}
        pairs = len(sources) // 2
        last = pairs - 1

        def weave_pair(p):
            grouped[p] = place(f"grouped{p}", half, BF16, 2 * p + 2, 1)[:]
            weave((2 * p, 2 * p + 1), grouped[p])

        def quantise_pair(p, host):
            if p >= 4:
                codes = host[:, 0 : 2 * P]
                scales = sbuf(f"scales{p}", 2 * P, U8)
                quantise(codes, scales[:], grouped[p], E4M3)
                for batch in range(2):
                    multiply(p - 4, batch, (codes.bitcast(E4M3), scales[:]), slice(batch * P, (batch + 1) * P), quantised[batch])
            elif p % 2 == 1:
                fmt = (E5M2, E4M3)[p // 2]
                codes = host[:, 0:N]
                scales = sbuf(f"scales{p}", N, U8)
                for h in range(2):
                    cols = slice(h * N // 2, (h + 1) * N // 2)
                    quantise(codes[:, cols], scales[:, cols], grouped[p - 1 + h], fmt)
                quantised[p // 2] = (codes.bitcast(fmt), scales[:])

        for p in range(pairs):
            cast(2 * p)
            if p in (3, 5, 6, 7):
                quantise_pair(p - 2, place(f"codes{p - 2}", N, U32, 2 * p, 0))
            gather_scalar(2 * p)
            if p >= 1:
                weave_pair(p - 1)
            gather_vector(2 * p + 1)
            if p < last:
                turn((2 * p, 2 * p + 1))

        emit(0, False, f"rounded{2 * last}")
        quantise_pair(last - 1, sbuf("codes_late", 2 * P, U32))
        for batch in range(2):
            i = 2 * last + batch
            turn((i,))
            grouped[i] = sbuf(f"grouped_last{batch}", P * PACK, BF16)
            weave((i,), grouped[i][:])
            codes = sbuf(f"codes_last{batch}", P, U32)
            scales = sbuf(f"scales_last{batch}", P, U8)
            quantise(codes[:], scales[:], grouped[i][:], E4M3)
            multiply(BLOCKS - 1, batch, (codes[:].bitcast(E4M3), scales[:]), slice(0, P), quantised[batch])
        emit(1, True, f"picked{2 * last + 1}")
        emit(2, False, "grouped_last1")
        emit(3, True)
